import numpy as np
import ml_dtypes


def mxq(x, axis, fmt="e4m3"):
    dtype, down = {"e4m3": (ml_dtypes.float8_e4m3fn, 7), "e5m2": (ml_dtypes.float8_e5m2, 14)}[fmt]
    v = np.moveaxis(np.asarray(x, np.float32).astype(ml_dtypes.bfloat16).astype(np.float64), axis, -1)
    blocks = v.reshape(v.shape[:-1] + (-1, 32))
    amax = np.abs(blocks).max(-1, keepdims=True)
    byte = np.maximum(np.where(amax > 0, np.frexp(amax)[1] - 1 + 127, 0) - down, 1)
    scale = np.exp2(byte - 127.0)
    codes = (blocks / scale).astype(np.float32).astype(dtype).astype(np.float64)
    return np.moveaxis((codes * scale).reshape(v.shape), -1, axis)


WIDE = False


def mx_kscale(k):
    if not WIDE:
        return np.ones(k)
    levels = np.array([10, -10, 5, -5, 0])
    if k % 512:
        return np.exp2(np.random.permutation(np.resize(levels, k // 32))).repeat(32)
    a = np.empty((k // 512, 16))
    for p in range(k // 512):
        a[p, :8] = np.random.permutation(np.resize(levels, 8))
        for g in range(8):
            far = levels[np.abs(levels - a[p, g]) >= 10]
            a[p, g + 8] = far[np.random.randint(len(far))]
    return np.exp2(a.ravel()).repeat(32)


def f64(x):
    return np.asarray(x).astype(np.float64)


def striped(idx):
    return np.tile(idx.reshape(-1, 16).T, (8, 1)).astype(np.uint16)


def unstriped(offs):
    return offs[:16].T.reshape(-1).astype(np.int64)


def pack_weight(w):
    k, n = w.shape
    w = f64(np.asarray(w, np.float32).astype(ml_dtypes.bfloat16)).reshape(k // 32, 32, n)
    amax = np.abs(w).max(1)
    byte = np.clip(np.where(amax > 0, np.frexp(amax)[1] - 1 + 127 - 7, 1), 1, 254)
    scaled = (w * np.exp2(127.0 - byte)[:, None, :]).reshape(k, n).astype(np.float32)
    words = np.ascontiguousarray(scaled.reshape(k // 512, 128, 4, n).transpose(0, 1, 3, 2)).astype(ml_dtypes.float8_e4m3fn).view(np.uint8)
    return words, np.ascontiguousarray(byte.astype(np.uint8).reshape(k // 512, 16, n))


def unpack_weight(words, scales):
    g, p, n, _ = words.shape
    vals = np.ascontiguousarray(words).view(ml_dtypes.float8_e4m3fn).astype(np.float64) * np.repeat(np.exp2(scales.astype(np.float64) - 127.0), 8, axis=1)[..., None]
    return vals.transpose(0, 1, 3, 2).reshape(g * 512, n)


E2M1 = np.array([0.0, 0.5, 1.0, 1.5, 2.0, 3.0, 4.0, 6.0, -0.0, -0.5, -1.0, -1.5, -2.0, -3.0, -4.0, -6.0])


def pack_fp4(w):
    k, n = w.shape
    w = f64(np.asarray(w, np.float32).astype(ml_dtypes.bfloat16)).reshape(k // 32, 32, n)
    amax = np.abs(w).max(1)
    mant, ex = np.frexp(amax / 6.0)
    byte = np.clip(np.where(amax > 0, np.where(mant > 0.5, ex, ex - 1) + 127, 1), 1, 254)
    scaled = (w * np.exp2(127.0 - byte)[:, None, :]).reshape(k, n).astype(np.float32)
    c = np.ascontiguousarray(scaled.reshape(k // 512, 128, 4, n).transpose(0, 1, 3, 2)).astype(ml_dtypes.float4_e2m1fn).view(np.uint8) & 0xF
    words = (c[..., 0::2] | (c[..., 1::2] << 4)).reshape(k // 512, 128, 2 * n)
    return np.ascontiguousarray(words), np.ascontiguousarray(byte.astype(np.uint8).reshape(k // 512, 16, n))


def unpack_fp4(words, scales):
    g, _, n = scales.shape
    words = np.ascontiguousarray(words).reshape(g, 128, n, 2)
    nib = np.empty((g, 128, n, 4), np.uint8)
    nib[..., 0::2] = words & 0xF
    nib[..., 1::2] = words >> 4
    vals = E2M1[nib] * np.repeat(np.exp2(scales.astype(np.float64) - 127.0), 8, axis=1)[..., None]
    return vals.transpose(0, 1, 3, 2).reshape(g * 512, n)


def planes(y):
    n, m = y.shape
    v = y.astype(np.float32).astype(ml_dtypes.bfloat16).astype(np.float64).reshape(n // 32, 32, m)
    top = np.abs(v).max(1)
    byte = np.clip(np.where(top > 0, np.frexp(top)[1] - 1 + 127 - 7, 1), 1, 254)
    codes = (v * np.exp2(127.0 - byte)[:, None, :]).reshape(n, m).astype(np.float32).astype(ml_dtypes.float8_e4m3fn).view(np.uint8)
    words = codes.reshape(n // 512, 128, 4, m).transpose(0, 1, 3, 2)
    return np.ascontiguousarray(words), np.ascontiguousarray(byte.astype(np.uint8).reshape(n // 512, 16, m))


def relu(v):
    return np.maximum(v, 0.0)


def sigmoid(v):
    return 1.0 / (1.0 + np.exp(-np.maximum(v, -700.0)))


K, T, S, H, Z, W = 512, 2048, 512, 512, 512, 2048
P = 2 ** 7


def setup_inputs():
    n = np.random.standard_normal
    s = mx_kscale(K)[:, None]
    u = mx_kscale(H)
    packed_xT = pack_weight(n((K, T)) * s)
    packed_w1 = pack_fp4(n((K, H)) / np.sqrt(K) / s)
    packed_w2 = pack_fp4(n((K, H)) / np.sqrt(K) / s)
    packed_eT = pack_weight(n((K, W)) * s)
    packed_w3 = pack_fp4(n((K, H)) / np.sqrt(K) / s)
    return {
        "x_words": packed_xT[0],
        "x_scales": packed_xT[1],
        "w1_words": packed_w1[0],
        "w1_scales": packed_w1[1],
        "w2_words": packed_w2[0],
        "w2_scales": packed_w2[1],
        "e_words": packed_eT[0],
        "e_scales": packed_eT[1],
        "w3_words": packed_w3[0],
        "w3_scales": packed_w3[1],
        "unit": (np.random.uniform(0.6, 1.4, (H, 1)) * u[:, None]).astype(np.float32),
        "unit2": (np.random.uniform(0.6, 1.4, (H, 1)) / np.sqrt(H) / u[:, None]).astype(np.float32),
        "dt": (np.tile(np.random.uniform(0.1, 1.5, W), (P, 1))).astype(np.float32),
        "offs": striped(np.random.permutation(T)[:S]),
        "tgt": striped(np.random.permutation(W)[:Z]),
        "ls": striped(np.random.permutation(S)),
        "neg_": striped(np.random.permutation(Z)),
    }


def reference(x_words, x_scales, w1_words, w1_scales, w2_words, w2_scales, e_words, e_scales, w3_words, w3_scales, unit, unit2, dt, offs, tgt, ls, neg_):
    xq = unpack_weight(x_words, x_scales)[:, unstriped(offs)]
    y = unpack_fp4(w1_words, w1_scales).T @ xq
    yg = unpack_fp4(w2_words, w2_scales).T @ xq
    yl = y[:, unstriped(ls)]
    upd = y * sigmoid(yg) + 0.5 * yl
    hid = f64(unit) * upd
    e_tgt = unpack_weight(e_words, e_scales)[:, unstriped(tgt)]
    ye = unpack_fp4(w3_words, w3_scales).T @ e_tgt
    tst = np.tanh(ye) + 0.3 * ye
    hid2 = f64(unit2) * tst
    sc = mxq(hid, 0, "e4m3").T @ mxq(hid2, 0, "e4m3")
    dec = sc * (np.exp(-1.0 * (f64(dt)[:1][:, unstriped(tgt)])))
    out_0 = dec - (0.7 * (relu(dec[:, unstriped(neg_)])))
    return (out_0,) + planes(out_0)

@@ -1,0 +1,250 @@
+from contextlib import ExitStack
+
+import concourse.mybir as mybir
+from concourse.masks import make_identity
+
+F32 = mybir.dt.float32
+BF16 = mybir.dt.bfloat16
+I32 = mybir.dt.int32
+U32 = mybir.dt.uint32
+U16 = mybir.dt.uint16
+U8 = mybir.dt.uint8
+FP8X4 = mybir.dt.float8_e4m3fn_x4
+FP4X4 = mybir.dt.float4_e2m1fn_x4
+ACT = mybir.ActivationFunctionType
+ALU = mybir.AluOpType
+
+P = 128
+PACK = 4
+TABLE = 2048
+PICKED = 512
+HALF = PICKED // 2
+LIST_COLS = PICKED // 16
+LS_PIECES = ((0, 384), (384, 512))
+LS_ON_VECTOR = ((0, 3),)
+NEG_PIECES = ((0, 256), (256, 384), (384, 512))
+FLOPS = 4 * 2 * 512 * 512 * 512
+
+
+def tile_picked_ylnkpr_lin_po_kernel(
+    tc, x_words, x_scales, w1_words, w1_scales, w2_words, w2_scales, e_words, e_scales, w3_words, w3_scales,
+    unit, unit2, dt, offs, tgt, ls, neg_, out_0, out_1, out_2,
+):
+    nc = tc.nc
+    with ExitStack() as ctx:
+        keep = ctx.enter_context(tc.tile_pool(name="keep", bufs=1))
+        psum = ctx.enter_context(tc.psum_pool(name="psum", bufs=8))
+
+        def sbuf(name, shape, dtype):
+            return keep.tile(shape, dtype, name=name, align_bytes=64)
+
+        def bank(name, shape):
+            return psum.tile(shape, F32, name=name, tag="bank")
+
+        def load_list(name, src):
+            tile = sbuf(name, [P, LIST_COLS], U16)
+            nc.sync.dma_start(tile[:], src)
+            return tile
+
+        def load_words(queue, name, src):
+            tile = keep.tile([P, TABLE], I32, name=name, tag=name, align_bytes=64)
+            queue.dma_start(tile[:], src[0].rearrange("p n t -> p (n t)").bitcast(I32))
+            return tile
+
+        def load_scale_rows(queue, tile, src):
+            for q in range(4):
+                queue.dma_start(tile[32 * q : 32 * q + 4, :].bitcast(I32), src[0, 4 * q : 4 * q + 4, :].bitcast(I32))
+
+        def zeroed_plane(engine, name, width):
+            tile = sbuf(name, [P, width], U8)
+            engine.memset(tile[:].bitcast(I32), 0)
+            return tile
+
+        def load_weight_words(name, src):
+            tile = sbuf(name, [P, 2 * PICKED], U8)
+            nc.gpsimd.dma_start(tile[:].bitcast(I32), src[0].bitcast(I32))
+            return tile
+
+        def deal(engine, name, raw, width):
+            tile = sbuf(name, [P, width], U8)
+            engine.tensor_copy(
+                tile[:].bitcast(I32).rearrange("p (t g q) -> p t g q", t=PACK, g=16),
+                raw[:].bitcast(I32).rearrange("p (g t q) -> p t g q", t=PACK, g=16),
+            )
+            return tile
+
+        def half_of(offsets, h):
+            return offsets[:, h * LIST_COLS // 2 : (h + 1) * LIST_COLS // 2]
+
+        e_plane = zeroed_plane(nc.vector, "e_plane", TABLE)
+        w3_plane = zeroed_plane(nc.vector, "w3_plane", PICKED)
+        x_plane = zeroed_plane(nc.vector, "x_plane", TABLE)
+        w1_plane = zeroed_plane(nc.vector, "w1_plane", PICKED)
+        w2_plane = zeroed_plane(nc.vector, "w2_plane", PICKED)
+        unit_rows = sbuf("unit_rows", [P, P], F32)
+        nc.vector.memset(unit_rows[:], 0.0)
+        ident = sbuf("ident", [P, P], F32)
+        make_identity(nc, ident[:])
+
+        tgt_list = load_list("tgt_list", tgt)
+        e_table = load_words(nc.scalar, "e_table", e_words)
+        offs_list = load_list("offs_list", offs)
+        ls_list = load_list("ls_list", ls)
+        neg_list = load_list("neg_list", neg_)
+        load_scale_rows(nc.sync, e_plane, e_scales)
+        load_scale_rows(nc.sync, w3_plane, w3_scales)
+        load_scale_rows(nc.sync, x_plane, x_scales)
+        load_scale_rows(nc.sync, w1_plane, w1_scales)
+        load_scale_rows(nc.sync, w2_plane, w2_scales)
+        w3_raw = load_weight_words("w3_raw", w3_words)
+        x_table = load_words(nc.gpsimd, "x_table", x_words)
+        for row, vec in ((4, unit2), (0, unit)):
+            nc.gpsimd.dma_start(
+                unit_rows[row : row + 4, :].rearrange("t (g r) -> t g r", r=8),
+                vec.rearrange("(g t r) o -> t g (r o)", t=PACK, r=8),
+            )
+        w1_raw = load_weight_words("w1_raw", w1_words)
+        w2_raw = load_weight_words("w2_raw", w2_words)
+
+        e_bytes = sbuf("e_bytes", [P, PICKED], U8)
+        nc.vector.tensor_copy(e_bytes[:], e_plane[:].indirect(tgt_list[:]))
+        e_codes = sbuf("e_codes", [P, PICKED], U32)
+        nc.vector.tensor_copy(e_codes[:], e_table[:].bitcast(U32).indirect(tgt_list[:]))
+        dt_table = keep.tile([P, TABLE], F32, name="dt_table", tag="e_table", align_bytes=64)
+        nc.sync.dma_start(dt_table[:], dt)
+        w3 = deal(nc.vector, "w3", w3_raw, 2 * PICKED)
+        w3_bytes = deal(nc.vector, "w3_bytes", w3_plane, PICKED)
+
+        unit_bank = bank("unit_bank", [P, P])
+        nc.tensor.transpose(unit_bank[:], unit_rows[:], ident[:])
+        half_unit = sbuf("half_unit", [P, PACK], F32)
+        nc.scalar.activation(half_unit[:], unit_bank[:, 0:4], ACT.Copy, scale=0.5)
+        unit2_cols = sbuf("unit2_cols", [P, PACK], F32)
+        nc.scalar.activation(unit2_cols[:], unit_bank[:, 4:8], ACT.Copy)
+
+        x_bytes = sbuf("x_bytes", [P, PICKED], U8)
+        nc.vector.tensor_copy(x_bytes[:], x_plane[:].indirect(offs_list[:]))
+        x_codes = sbuf("x_codes", [P, PICKED], U32)
+        nc.vector.tensor_copy(x_codes[:], x_table[:].bitcast(U32).indirect(offs_list[:]))
+        w1 = deal(nc.gpsimd, "w1", w1_raw, 2 * PICKED)
+        w1_bytes = deal(nc.gpsimd, "w1_bytes", w1_plane, PICKED)
+        w2 = deal(nc.gpsimd, "w2", w2_raw, 2 * PICKED)
+        w2_bytes = deal(nc.gpsimd, "w2_bytes", w2_plane, PICKED)
+
+        def weight_pass(out, words, scale_bytes, t, codes, code_bytes):
+            nc.tensor.matmul_mx(
+                out=out,
+                lhsT=words[:, 2 * P * t : 2 * P * (t + 1)].bitcast(FP4X4),
+                lhsT_scale=scale_bytes[:, P * t : P * (t + 1)],
+                rhs=codes.bitcast(FP8X4),
+                rhs_scale=code_bytes,
+                start=True,
+                stop=True,
+            )
+
+        tanh_ye = sbuf("tanh_ye", [P, PICKED, PACK], F32)
+        tst = keep.tile([P, PICKED, PACK], F32, name="tst", tag="x_table", align_bytes=64)
+        hid2 = sbuf("hid2", [P, PICKED, PACK], BF16)
+        for b in range(4):
+            cols = slice(P * b, P * (b + 1))
+            ye = bank("ye", [P, PACK, P])
+            for t in range(PACK):
+                weight_pass(ye[:, t, :], w3, w3_bytes, t, e_codes[:, cols], e_bytes[:, cols])
+            woven = ye[:].rearrange("p t n -> p n t")
+            nc.scalar.activation(tanh_ye[:, cols, :], woven, ACT.Tanh)
+            nc.vector.scalar_tensor_tensor(tst[:, cols, :], woven, 0.3, tanh_ye[:, cols, :], ALU.mult, ALU.add)
+        hid2_codes = sbuf("hid2_codes", [P, PICKED], U32)
+        hid2_bytes = sbuf("hid2_bytes", [P, PICKED], U8)
+        for h in range(2):
+            cols = slice(HALF * h, HALF * (h + 1))
+            nc.vector.tensor_tensor(
+                hid2[:, cols, :], tst[:, cols, :], unit2_cols[:].unsqueeze(1).to_broadcast([P, HALF, PACK]), ALU.mult
+            )
+        nc.vector.quantize_mx(
+            out=hid2_codes[:].bitcast(FP8X4), scales=hid2_bytes[:], in_=hid2[:].rearrange("p e t -> p (e t)")
+        )
+
+        gated = sbuf("gated", [P, PACK, PICKED], F32)
+        y_rows = []
+        for t in range(PACK):
+            y = bank("y", [P, PICKED])
+            weight_pass(y[:], w1, w1_bytes, t, x_codes[:], x_bytes[:])
+            yg = bank("yg", [P, PICKED])
+            weight_pass(yg[:], w2, w2_bytes, t, x_codes[:], x_bytes[:])
+            y_row = keep.tile([P, PICKED], F32, name=f"y_row{t}", tag=f"y_row{t}", align_bytes=64)
+            nc.scalar.activation(y_row[:], y[:], ACT.Copy, scale=half_unit[:, t : t + 1])
+            tanh_yg = sbuf(f"tanh_yg{t}", [P, PICKED], F32)
+            nc.scalar.activation(tanh_yg[:], yg[:], ACT.Tanh, scale=0.5)
+            nc.vector.scalar_tensor_tensor(gated[:, t, :], tanh_yg[:], 1.0, y_row[:], ALU.add, ALU.mult)
+            y_rows.append(y_row)
+
+        y_other = sbuf("y_other", [P, PACK, PICKED], F32)
+        hid = sbuf("hid", [P, PACK, P, PACK], BF16)
+        for lo, hi in LS_PIECES:
+            cols = slice(lo, hi)
+            for t in range(PACK):
+                window = y_rows[t][:].indirect(ls_list[:, lo // 16 : hi // 16])
+                if (lo, t) in LS_ON_VECTOR:
+                    nc.vector.tensor_copy(y_other[:, t, cols], window)
+                else:
+                    nc.scalar.activation(y_other[:, t, cols], window, ACT.Copy)
+            nc.vector.tensor_tensor(
+                hid[:, :, lo // PACK : hi // PACK, :].rearrange("p r m t -> p m r t"),
+                gated[:, :, cols].rearrange("p t (m r) -> p m r t", r=PACK),
+                y_other[:, :, cols].rearrange("p t (m r) -> p m r t", r=PACK),
+                ALU.add,
+            )
+
+        fade = keep.tile([P, PICKED], F32, name="fade", tag="y_row2", align_bytes=64)
+        nc.scalar.activation(fade[:], dt_table[:].indirect(tgt_list[:]), ACT.Exp, scale=-1.0)
+
+        hid_codes = sbuf("hid_codes", [P, PICKED], U32)
+        hid_bytes = sbuf("hid_bytes", [P, PICKED], U8)
+        for r in range(PACK):
+            cols = slice(P * r, P * (r + 1))
+            nc.vector.quantize_mx(
+                out=hid_codes[:, cols].bitcast(FP8X4),
+                scales=hid_bytes[:, cols],
+                in_=hid[:, r, :, :].rearrange("p m t -> p (m t)"),
+            )
+        dec_rows = []
+        for r in range(PACK):
+            cols = slice(P * r, P * (r + 1))
+            sc = bank("sc", [P, PICKED])
+            nc.tensor.matmul_mx(
+                out=sc[:],
+                lhsT=hid_codes[:, cols].bitcast(FP8X4),
+                lhsT_scale=hid_bytes[:, cols],
+                rhs=hid2_codes[:].bitcast(FP8X4),
+                rhs_scale=hid2_bytes[:],
+                start=True,
+                stop=True,
+            )
+            dec = sbuf(f"dec{r}", [P, PICKED], F32)
+            nc.vector.tensor_tensor(dec[:], sc[:], fade[:], ALU.mult)
+            dec_rows.append(dec)
+
+        out_rows = out_0.rearrange("(p r) e -> p r e", r=PACK)
+        out_words = out_1[0].rearrange("p n t -> p (n t)").bitcast(I32)
+        out_codes = sbuf("out_codes", [P, PICKED], U32)
+        out_bytes = sbuf("out_bytes", [P, PICKED], U8)
+        for lo, hi in NEG_PIECES:
+            cols = slice(lo, hi)
+            pull = sbuf(f"pull{lo}", [P, PACK, hi - lo], F32)
+            result = sbuf(f"result{lo}", [P, PACK, hi - lo], F32)
+            for r in range(PACK):
+                window = dec_rows[r][:].indirect(neg_list[:, lo // 16 : hi // 16])
+                nc.scalar.activation(pull[:, r, :], window, ACT.Copy, scale=-0.7)
+                nc.vector.scalar_tensor_tensor(result[:, r, :], pull[:, r, :], 0.0, dec_rows[r][:, cols], ALU.min, ALU.add)
+            nc.sync.dma_start(out_rows[:, :, cols], result[:])
+            rounded = sbuf(f"rounded{lo}", [P, hi - lo, PACK], BF16)
+            nc.vector.tensor_copy(rounded[:], result[:].rearrange("p r e -> p e r"))
+            nc.vector.quantize_mx(
+                out=out_codes[:, cols].bitcast(FP8X4),
+                scales=out_bytes[:, cols],
+                in_=rounded[:].rearrange("p e r -> p (e r)"),
+            )
+            nc.sync.dma_start(out_words[:, cols], out_codes[:, cols].bitcast(I32))
+        for q in range(4):
+            queue = nc.sync if q % 2 == 0 else nc.scalar
+            queue.dma_start(out_2[0, 4 * q : 4 * q + 4, :].bitcast(I32), out_bytes[32 * q : 32 * q + 4, :].bitcast(I32))

@@ -20,9 +20,9 @@ TABLE = 2048
 PICKED = 512
 HALF = PICKED // 2
 LIST_COLS = PICKED // 16
-LS_PIECES = ((0, 384), (384, 512))
-LS_ON_VECTOR = ((0, 3),)
-NEG_PIECES = ((0, 256), (256, 384), (384, 512))
+LS_PIECES = ((0, 320), (320, 512))
+LS_ON_VECTOR = ((0, 3), (320, 3))
+OUT_SPLIT = 160
 FLOPS = 4 * 2 * 512 * 512 * 512
 
 
@@ -200,14 +200,14 @@ def tile_picked_ylnkpr_lin_po_kernel(
 
         hid_codes = sbuf("hid_codes", [P, PICKED], U32)
         hid_bytes = sbuf("hid_bytes", [P, PICKED], U8)
-        for r in range(PACK):
-            cols = slice(P * r, P * (r + 1))
+        for h in range(2):
+            cols = slice(HALF * h, HALF * (h + 1))
             nc.vector.quantize_mx(
                 out=hid_codes[:, cols].bitcast(FP8X4),
                 scales=hid_bytes[:, cols],
-                in_=hid[:, r, :, :].rearrange("p m t -> p (m t)"),
+                in_=hid[:, 2 * h : 2 * h + 2, :, :].rearrange("p r m t -> p (r m t)"),
             )
-        dec_rows = []
+        dec = sbuf("dec", [P, PACK, PICKED], F32)
         for r in range(PACK):
             cols = slice(P * r, P * (r + 1))
             sc = bank("sc", [P, PICKED])
@@ -220,25 +220,35 @@ def tile_picked_ylnkpr_lin_po_kernel(
                 start=True,
                 stop=True,
             )
-            dec = sbuf(f"dec{r}", [P, PICKED], F32)
-            nc.vector.tensor_tensor(dec[:], sc[:], fade[:], ALU.mult)
-            dec_rows.append(dec)
+            nc.vector.tensor_tensor(dec[:, r, :], sc[:], fade[:], ALU.mult)
 
         out_rows = out_0.rearrange("(p r) e -> p r e", r=PACK)
         out_words = out_1[0].rearrange("p n t -> p (n t)").bitcast(I32)
         out_codes = sbuf("out_codes", [P, PICKED], U32)
         out_bytes = sbuf("out_bytes", [P, PICKED], U8)
-        for lo, hi in NEG_PIECES:
-            cols = slice(lo, hi)
-            pull = sbuf(f"pull{lo}", [P, PACK, hi - lo], F32)
-            result = sbuf(f"result{lo}", [P, PACK, hi - lo], F32)
+        for h in range(2):
+            cols = slice(HALF * h, HALF * (h + 1))
+            pull = sbuf(f"pull{h}", [P, PACK, HALF], F32)
+            result = sbuf(f"result{h}", [P, PACK, HALF], F32)
             for r in range(PACK):
-                window = dec_rows[r][:].indirect(neg_list[:, lo // 16 : hi // 16])
-                nc.scalar.activation(pull[:, r, :], window, ACT.Copy, scale=-0.7)
-                nc.vector.scalar_tensor_tensor(result[:, r, :], pull[:, r, :], 0.0, dec_rows[r][:, cols], ALU.min, ALU.add)
-            nc.sync.dma_start(out_rows[:, :, cols], result[:])
-            rounded = sbuf(f"rounded{lo}", [P, hi - lo, PACK], BF16)
-            nc.vector.tensor_copy(rounded[:], result[:].rearrange("p r e -> p e r"))
+                nc.scalar.activation(pull[:, r, :], dec[:, r, :].indirect(half_of(neg_list, h)), ACT.Copy, scale=-0.7)
+                if r % 2 == 1:
+                    pair = slice(r - 1, r + 1)
+                    nc.vector.scalar_tensor_tensor(
+                        result[:, pair, :], pull[:, pair, :], 0.0, dec[:, pair, cols], ALU.min, ALU.add
+                    )
+                    nc.sync.dma_start(out_rows[:, pair, cols], result[:, pair, :])
+            rounded = sbuf(f"rounded{h}", [P, HALF, PACK], BF16)
+            split = HALF if h == 0 else OUT_SPLIT
+            nc.vector.tensor_copy(
+                rounded[:, :split, :].rearrange("p (c i) r -> p c r i", i=4),
+                result[:, :, :split].rearrange("p r (c i) -> p c r i", i=4),
+            )
+            if split < HALF:
+                nc.scalar.copy(
+                    rounded[:, split:, :].rearrange("p (c i) r -> p c r i", i=4),
+                    result[:, :, split:].rearrange("p r (c i) -> p c r i", i=4),
+                )
             nc.vector.quantize_mx(
                 out=out_codes[:, cols].bitcast(FP8X4),
                 scales=out_bytes[:, cols],

from contextlib import ExitStack

import concourse.mybir as mybir
from concourse.masks import make_identity

F32 = mybir.dt.float32
BF16 = mybir.dt.bfloat16
I32 = mybir.dt.int32
U32 = mybir.dt.uint32
U16 = mybir.dt.uint16
U8 = mybir.dt.uint8
FP8X4 = mybir.dt.float8_e4m3fn_x4
FP4X4 = mybir.dt.float4_e2m1fn_x4
ACT = mybir.ActivationFunctionType
ALU = mybir.AluOpType

P = 128
PACK = 4
TABLE = 2048
PICKED = 512
HALF = PICKED // 2
LIST_COLS = PICKED // 16
LS_PIECES = ((0, 320), (320, 512))
LS_ON_VECTOR = ((0, 3), (320, 3))
OUT_SPLIT = 160
FLOPS = 4 * 2 * 512 * 512 * 512


def tile_picked_ylnkpr_lin_po_kernel(
    tc, x_words, x_scales, w1_words, w1_scales, w2_words, w2_scales, e_words, e_scales, w3_words, w3_scales,
    unit, unit2, dt, offs, tgt, ls, neg_, out_0, out_1, out_2,
):
    nc = tc.nc
    with ExitStack() as ctx:
        keep = ctx.enter_context(tc.tile_pool(name="keep", bufs=1))
        psum = ctx.enter_context(tc.psum_pool(name="psum", bufs=8))

        def sbuf(name, shape, dtype):
            return keep.tile(shape, dtype, name=name, align_bytes=64)

        def bank(name, shape):
            return psum.tile(shape, F32, name=name, tag="bank")

        def load_list(name, src):
            tile = sbuf(name, [P, LIST_COLS], U16)
            nc.sync.dma_start(tile[:], src)
            return tile

        def load_words(queue, name, src):
            tile = keep.tile([P, TABLE], I32, name=name, tag=name, align_bytes=64)
            queue.dma_start(tile[:], src[0].rearrange("p n t -> p (n t)").bitcast(I32))
            return tile

        def load_scale_rows(queue, tile, src):
            for q in range(4):
                queue.dma_start(tile[32 * q : 32 * q + 4, :].bitcast(I32), src[0, 4 * q : 4 * q + 4, :].bitcast(I32))

        def zeroed_plane(engine, name, width):
            tile = sbuf(name, [P, width], U8)
            engine.memset(tile[:].bitcast(I32), 0)
            return tile

        def load_weight_words(name, src):
            tile = sbuf(name, [P, 2 * PICKED], U8)
            nc.gpsimd.dma_start(tile[:].bitcast(I32), src[0].bitcast(I32))
            return tile

        def deal(engine, name, raw, width):
            tile = sbuf(name, [P, width], U8)
            engine.tensor_copy(
                tile[:].bitcast(I32).rearrange("p (t g q) -> p t g q", t=PACK, g=16),
                raw[:].bitcast(I32).rearrange("p (g t q) -> p t g q", t=PACK, g=16),
            )
            return tile

        def half_of(offsets, h):
            return offsets[:, h * LIST_COLS // 2 : (h + 1) * LIST_COLS // 2]

        e_plane = zeroed_plane(nc.vector, "e_plane", TABLE)
        w3_plane = zeroed_plane(nc.vector, "w3_plane", PICKED)
        x_plane = zeroed_plane(nc.vector, "x_plane", TABLE)
        w1_plane = zeroed_plane(nc.vector, "w1_plane", PICKED)
        w2_plane = zeroed_plane(nc.vector, "w2_plane", PICKED)
        unit_rows = sbuf("unit_rows", [P, P], F32)
        nc.vector.memset(unit_rows[:], 0.0)
        ident = sbuf("ident", [P, P], F32)
        make_identity(nc, ident[:])

        tgt_list = load_list("tgt_list", tgt)
        e_table = load_words(nc.scalar, "e_table", e_words)
        offs_list = load_list("offs_list", offs)
        ls_list = load_list("ls_list", ls)
        neg_list = load_list("neg_list", neg_)
        load_scale_rows(nc.sync, e_plane, e_scales)
        load_scale_rows(nc.sync, w3_plane, w3_scales)
        load_scale_rows(nc.sync, x_plane, x_scales)
        load_scale_rows(nc.sync, w1_plane, w1_scales)
        load_scale_rows(nc.sync, w2_plane, w2_scales)
        w3_raw = load_weight_words("w3_raw", w3_words)
        x_table = load_words(nc.gpsimd, "x_table", x_words)
        for row, vec in ((4, unit2), (0, unit)):
            nc.gpsimd.dma_start(
                unit_rows[row : row + 4, :].rearrange("t (g r) -> t g r", r=8),
                vec.rearrange("(g t r) o -> t g (r o)", t=PACK, r=8),
            )
        w1_raw = load_weight_words("w1_raw", w1_words)
        w2_raw = load_weight_words("w2_raw", w2_words)

        e_bytes = sbuf("e_bytes", [P, PICKED], U8)
        nc.vector.tensor_copy(e_bytes[:], e_plane[:].indirect(tgt_list[:]))
        e_codes = sbuf("e_codes", [P, PICKED], U32)
        nc.vector.tensor_copy(e_codes[:], e_table[:].bitcast(U32).indirect(tgt_list[:]))
        dt_table = keep.tile([P, TABLE], F32, name="dt_table", tag="e_table", align_bytes=64)
        nc.sync.dma_start(dt_table[:], dt)
        w3 = deal(nc.vector, "w3", w3_raw, 2 * PICKED)
        w3_bytes = deal(nc.vector, "w3_bytes", w3_plane, PICKED)

        unit_bank = bank("unit_bank", [P, P])
        nc.tensor.transpose(unit_bank[:], unit_rows[:], ident[:])
        half_unit = sbuf("half_unit", [P, PACK], F32)
        nc.scalar.activation(half_unit[:], unit_bank[:, 0:4], ACT.Copy, scale=0.5)
        unit2_cols = sbuf("unit2_cols", [P, PACK], F32)
        nc.scalar.activation(unit2_cols[:], unit_bank[:, 4:8], ACT.Copy)

        x_bytes = sbuf("x_bytes", [P, PICKED], U8)
        nc.vector.tensor_copy(x_bytes[:], x_plane[:].indirect(offs_list[:]))
        x_codes = sbuf("x_codes", [P, PICKED], U32)
        nc.vector.tensor_copy(x_codes[:], x_table[:].bitcast(U32).indirect(offs_list[:]))
        w1 = deal(nc.gpsimd, "w1", w1_raw, 2 * PICKED)
        w1_bytes = deal(nc.gpsimd, "w1_bytes", w1_plane, PICKED)
        w2 = deal(nc.gpsimd, "w2", w2_raw, 2 * PICKED)
        w2_bytes = deal(nc.gpsimd, "w2_bytes", w2_plane, PICKED)

        def weight_pass(out, words, scale_bytes, t, codes, code_bytes):
            nc.tensor.matmul_mx(
                out=out,
                lhsT=words[:, 2 * P * t : 2 * P * (t + 1)].bitcast(FP4X4),
                lhsT_scale=scale_bytes[:, P * t : P * (t + 1)],
                rhs=codes.bitcast(FP8X4),
                rhs_scale=code_bytes,
                start=True,
                stop=True,
            )

        tanh_ye = sbuf("tanh_ye", [P, PICKED, PACK], F32)
        tst = keep.tile([P, PICKED, PACK], F32, name="tst", tag="x_table", align_bytes=64)
        hid2 = sbuf("hid2", [P, PICKED, PACK], BF16)
        for b in range(4):
            cols = slice(P * b, P * (b + 1))
            ye = bank("ye", [P, PACK, P])
            for t in range(PACK):
                weight_pass(ye[:, t, :], w3, w3_bytes, t, e_codes[:, cols], e_bytes[:, cols])
            woven = ye[:].rearrange("p t n -> p n t")
            nc.scalar.activation(tanh_ye[:, cols, :], woven, ACT.Tanh)
            nc.vector.scalar_tensor_tensor(tst[:, cols, :], woven, 0.3, tanh_ye[:, cols, :], ALU.mult, ALU.add)
        hid2_codes = sbuf("hid2_codes", [P, PICKED], U32)
        hid2_bytes = sbuf("hid2_bytes", [P, PICKED], U8)
        for h in range(2):
            cols = slice(HALF * h, HALF * (h + 1))
            nc.vector.tensor_tensor(
                hid2[:, cols, :], tst[:, cols, :], unit2_cols[:].unsqueeze(1).to_broadcast([P, HALF, PACK]), ALU.mult
            )
        nc.vector.quantize_mx(
            out=hid2_codes[:].bitcast(FP8X4), scales=hid2_bytes[:], in_=hid2[:].rearrange("p e t -> p (e t)")
        )

        gated = sbuf("gated", [P, PACK, PICKED], F32)
        y_rows = []
        for t in range(PACK):
            y = bank("y", [P, PICKED])
            weight_pass(y[:], w1, w1_bytes, t, x_codes[:], x_bytes[:])
            yg = bank("yg", [P, PICKED])
            weight_pass(yg[:], w2, w2_bytes, t, x_codes[:], x_bytes[:])
            y_row = keep.tile([P, PICKED], F32, name=f"y_row{t}", tag=f"y_row{t}", align_bytes=64)
            nc.scalar.activation(y_row[:], y[:], ACT.Copy, scale=half_unit[:, t : t + 1])
            tanh_yg = sbuf(f"tanh_yg{t}", [P, PICKED], F32)
            nc.scalar.activation(tanh_yg[:], yg[:], ACT.Tanh, scale=0.5)
            nc.vector.scalar_tensor_tensor(gated[:, t, :], tanh_yg[:], 1.0, y_row[:], ALU.add, ALU.mult)
            y_rows.append(y_row)

        y_other = sbuf("y_other", [P, PACK, PICKED], F32)
        hid = sbuf("hid", [P, PACK, P, PACK], BF16)
        for lo, hi in LS_PIECES:
            cols = slice(lo, hi)
            for t in range(PACK):
                window = y_rows[t][:].indirect(ls_list[:, lo // 16 : hi // 16])
                if (lo, t) in LS_ON_VECTOR:
                    nc.vector.tensor_copy(y_other[:, t, cols], window)
                else:
                    nc.scalar.activation(y_other[:, t, cols], window, ACT.Copy)
            nc.vector.tensor_tensor(
                hid[:, :, lo // PACK : hi // PACK, :].rearrange("p r m t -> p m r t"),
                gated[:, :, cols].rearrange("p t (m r) -> p m r t", r=PACK),
                y_other[:, :, cols].rearrange("p t (m r) -> p m r t", r=PACK),
                ALU.add,
            )

        fade = keep.tile([P, PICKED], F32, name="fade", tag="y_row2", align_bytes=64)
        nc.scalar.activation(fade[:], dt_table[:].indirect(tgt_list[:]), ACT.Exp, scale=-1.0)

        hid_codes = sbuf("hid_codes", [P, PICKED], U32)
        hid_bytes = sbuf("hid_bytes", [P, PICKED], U8)
        for h in range(2):
            cols = slice(HALF * h, HALF * (h + 1))
            nc.vector.quantize_mx(
                out=hid_codes[:, cols].bitcast(FP8X4),
                scales=hid_bytes[:, cols],
                in_=hid[:, 2 * h : 2 * h + 2, :, :].rearrange("p r m t -> p (r m t)"),
            )
        dec = sbuf("dec", [P, PACK, PICKED], F32)
        for r in range(PACK):
            cols = slice(P * r, P * (r + 1))
            sc = bank("sc", [P, PICKED])
            nc.tensor.matmul_mx(
                out=sc[:],
                lhsT=hid_codes[:, cols].bitcast(FP8X4),
                lhsT_scale=hid_bytes[:, cols],
                rhs=hid2_codes[:].bitcast(FP8X4),
                rhs_scale=hid2_bytes[:],
                start=True,
                stop=True,
            )
            nc.vector.tensor_tensor(dec[:, r, :], sc[:], fade[:], ALU.mult)

        out_rows = out_0.rearrange("(p r) e -> p r e", r=PACK)
        out_words = out_1[0].rearrange("p n t -> p (n t)").bitcast(I32)
        out_codes = sbuf("out_codes", [P, PICKED], U32)
        out_bytes = sbuf("out_bytes", [P, PICKED], U8)
        for h in range(2):
            cols = slice(HALF * h, HALF * (h + 1))
            pull = sbuf(f"pull{h}", [P, PACK, HALF], F32)
            result = sbuf(f"result{h}", [P, PACK, HALF], F32)
            for r in range(PACK):
                nc.scalar.activation(pull[:, r, :], dec[:, r, :].indirect(half_of(neg_list, h)), ACT.Copy, scale=-0.7)
                if r % 2 == 1:
                    pair = slice(r - 1, r + 1)
                    nc.vector.scalar_tensor_tensor(
                        result[:, pair, :], pull[:, pair, :], 0.0, dec[:, pair, cols], ALU.min, ALU.add
                    )
                    nc.sync.dma_start(out_rows[:, pair, cols], result[:, pair, :])
            rounded = sbuf(f"rounded{h}", [P, HALF, PACK], BF16)
            split = HALF if h == 0 else OUT_SPLIT
            nc.vector.tensor_copy(
                rounded[:, :split, :].rearrange("p (c i) r -> p c r i", i=4),
                result[:, :, :split].rearrange("p r (c i) -> p c r i", i=4),
            )
            if split < HALF:
                nc.scalar.copy(
                    rounded[:, split:, :].rearrange("p (c i) r -> p c r i", i=4),
                    result[:, :, split:].rearrange("p r (c i) -> p c r i", i=4),
                )
            nc.vector.quantize_mx(
                out=out_codes[:, cols].bitcast(FP8X4),
                scales=out_bytes[:, cols],
                in_=rounded[:].rearrange("p e r -> p (e r)"),
            )
            nc.sync.dma_start(out_words[:, cols], out_codes[:, cols].bitcast(I32))
        for q in range(4):
            queue = nc.sync if q % 2 == 0 else nc.scalar
            queue.dma_start(out_2[0, 4 * q : 4 * q + 4, :].bitcast(I32), out_bytes[32 * q : 32 * q + 4, :].bitcast(I32))
